import numpy as np
import ml_dtypes


def mxq(x, axis, fmt="e4m3"):
    dtype, down = {"e4m3": (ml_dtypes.float8_e4m3fn, 7), "e5m2": (ml_dtypes.float8_e5m2, 14)}[fmt]
    v = np.moveaxis(np.asarray(x, np.float32).astype(ml_dtypes.bfloat16).astype(np.float64), axis, -1)
    blocks = v.reshape(v.shape[:-1] + (-1, 32))
    amax = np.abs(blocks).max(-1, keepdims=True)
    byte = np.maximum(np.where(amax > 0, np.frexp(amax)[1] - 1 + 127, 0) - down, 1)
    scale = np.exp2(byte - 127.0)
    codes = (blocks / scale).astype(np.float32).astype(dtype).astype(np.float64)
    return np.moveaxis((codes * scale).reshape(v.shape), -1, axis)


WIDE = False


def mx_kscale(k):
    if not WIDE:
        return np.ones(k)
    levels = np.array([10, -10, 5, -5, 0])
    if k % 512:
        return np.exp2(np.random.permutation(np.resize(levels, k // 32))).repeat(32)
    a = np.empty((k // 512, 16))
    for p in range(k // 512):
        a[p, :8] = np.random.permutation(np.resize(levels, 8))
        for g in range(8):
            far = levels[np.abs(levels - a[p, g]) >= 10]
            a[p, g + 8] = far[np.random.randint(len(far))]
    return np.exp2(a.ravel()).repeat(32)


def f64(x):
    return np.asarray(x).astype(np.float64)


def striped(idx):
    return np.tile(idx.reshape(-1, 16).T, (8, 1)).astype(np.uint16)


def unstriped(offs):
    return offs[:16].T.reshape(-1).astype(np.int64)


E2M1 = np.array([0.0, 0.5, 1.0, 1.5, 2.0, 3.0, 4.0, 6.0, -0.0, -0.5, -1.0, -1.5, -2.0, -3.0, -4.0, -6.0])


def pack_weight(w, fmt):
    k, n = w.shape
    w = f64(np.asarray(w, np.float32).astype(ml_dtypes.bfloat16)).reshape(k // 32, 32, n)
    amax = np.abs(w).max(1)
    if fmt == "e4m3":
        byte = np.frexp(amax)[1] - 1 + 127 - 7
    else:
        mant, ex = np.frexp(amax / 6.0)
        byte = np.where(mant > 0.5, ex, ex - 1) + 127
    byte = np.clip(np.where(amax > 0, byte, 1), 1, 254)
    scaled = (w * np.exp2(127.0 - byte)[:, None, :]).reshape(k, n).astype(np.float32)
    by_word = np.ascontiguousarray(scaled.reshape(k // 512, 128, 4, n).transpose(0, 1, 3, 2))
    if fmt == "e4m3":
        words = by_word.astype(ml_dtypes.float8_e4m3fn).view(np.uint8)
    else:
        c = by_word.astype(ml_dtypes.float4_e2m1fn).view(np.uint8) & 0xF
        words = (c[..., 0::2] | (c[..., 1::2] << 4)).reshape(k // 512, 128, 2 * n)
    return np.ascontiguousarray(words), np.ascontiguousarray(byte.astype(np.uint8).reshape(k // 512, 16, n))


def unpack_weight(words, scales, fmt):
    g, _, n = scales.shape
    words = np.ascontiguousarray(words).reshape(g, 128, n, -1)
    if fmt == "e4m3":
        vals = words.view(ml_dtypes.float8_e4m3fn).astype(np.float64)
    else:
        nib = np.empty((g, 128, n, 4), np.uint8)
        nib[..., 0::2] = words & 0xF
        nib[..., 1::2] = words >> 4
        vals = E2M1[nib]
    vals = vals * np.repeat(np.exp2(scales.astype(np.float64) - 127.0), 8, axis=1)[..., None]
    return vals.transpose(0, 1, 3, 2).reshape(g * 512, n)


def relu(v):
    return np.maximum(v, 0.0)


K, T, E, C, N = 512, 1024, 8, 256, 384


def by_expert(wq, xq):
    return np.concatenate([wq[e].T @ xq[:, e * C:(e + 1) * C] for e in range(E)], axis=1)


def setup_inputs():
    n = np.random.standard_normal
    s = mx_kscale(K)[:, None]
    first = np.random.permutation(np.repeat(np.arange(E), T // E))
    second = (first + 1 + np.random.permutation(np.repeat(np.arange(E - 1), -(-T // (E - 1)))[:T])) % E
    while np.bincount(second, minlength=E).max() != T // E:
        load = np.bincount(second, minlength=E); hi, lo = int(load.argmax()), int(load.argmin())
        t = np.flatnonzero((second == hi) & (first != lo))[0]; second[t] = lo
    slot_token = np.empty(E * C, np.int64); pos = np.empty((2, T), np.int64); fill = np.zeros(E, np.int64)
    place = np.stack([np.random.permutation(C) for _ in range(E)])
    for r, deal in enumerate((first, second)):
        for t in np.random.permutation(T):
            e = deal[t]; j = e * C + place[e, fill[e]]; fill[e] += 1; slot_token[j] = t; pos[r, t] = j
    g = np.random.uniform(0.2, 0.8, T)
    x = pack_weight(n((K, T)) * s, "e4m3")
    return {
        "x_words": x[0],
        "x_scales": x[1],
        "w": (n((E, K, N)) / np.sqrt(K) / s[None]).astype(np.float32),
        "b": (0.3 * n((N, E))).astype(np.float32),
        "gate": np.stack([np.tile(g, (N, 1)), np.tile(1.0 - g, (N, 1))]).astype(np.float32),
        "offs": striped(slot_token),
        "pos1": striped(pos[0]),
        "pos2": striped(pos[1]),
    }


def reference(x_words, x_scales, w, b, gate, offs, pos1, pos2):
    idx = unstriped(offs)
    xq = unpack_weight(x_words, x_scales, "e4m3")[:, idx]
    y = by_expert(mxq(f64(w), 1, "e4m3"), xq)
    y = relu(y + np.repeat(f64(b), C, axis=1))
    return f64(gate[0]) * y[:, unstriped(pos1)] + f64(gate[1]) * y[:, unstriped(pos2)]

@@ -1,0 +1,153 @@
+from contextlib import ExitStack
+
+import concourse.mybir as mybir
+
+K, T, E, C, N = 512, 1024, 8, 256, 384
+S = E * C
+P = 128
+NB = N // P
+FLOPS = 2 * K * N * S
+BYTES = K * T + 16 * T + 4 * E * K * N + 4 * N * E + 4 * 2 * T + 2 * (S + 2 * T) + 4 * N * T
+
+F32 = mybir.dt.float32
+BF16 = mybir.dt.bfloat16
+I32 = mybir.dt.int32
+U32 = mybir.dt.uint32
+U16 = mybir.dt.uint16
+U8 = mybir.dt.uint8
+FP8X4 = mybir.dt.float8_e4m3fn_x4
+MULT = mybir.AluOpType.mult
+ADD = mybir.AluOpType.add
+RELU = mybir.ActivationFunctionType.Relu
+
+GATHER = 512
+HALF = 512
+
+
+def tile_moe_pkd_lin_relu_kernel(tc, x_words, x_scales, w, b, gate, offs, pos1, pos2, out):
+    nc = tc.nc
+    with ExitStack() as ctx:
+        lists = ctx.enter_context(tc.tile_pool(name="lists", bufs=1))
+        keep = ctx.enter_context(tc.tile_pool(name="keep", bufs=1))
+        psum = ctx.enter_context(tc.psum_pool(name="psum", bufs=8))
+
+        offs_t = lists.tile([P, S // 16], U16, name="offs_t")
+        pos_t = [lists.tile([P, T // 16], U16, name="pos%d_t" % r) for r in range(2)]
+        xw = keep.tile([P, T], I32, name="xw", align_bytes=64)
+        xs = keep.tile([P, T], U8, name="xs", align_bytes=64)
+        bias = keep.tile([P, NB, E], F32, name="bias")
+        gates = [keep.tile([P, T], F32, name="gate%d" % r) for r in range(2)]
+
+        nc.gpsimd.memset(xs[:].bitcast(I32), 0)
+        nc.sync.dma_start(offs_t[:], offs)
+        for q in range(4):
+            nc.sync.dma_start(out=xs[32 * q : 32 * q + 4, :].bitcast(I32), in_=x_scales[0, 4 * q : 4 * q + 4, :].bitcast(I32))
+        nc.sync.dma_start(out=xw[:], in_=x_words[0].rearrange("p t r -> p (t r)").bitcast(I32))
+
+        raw = {}
+
+        def load_w(e, nb0, nb1):
+            width = (nb1 - nb0) * P
+            tag = "y0" if (e, nb0) == (E // 2, 0) else "raw%d_%d" % (e, nb0)
+            t = keep.tile([P, 4, width], F32, name="raw%d_%d" % (e, nb0), tag=tag)
+            nc.sync.dma_start(out=t[:], in_=w[e, :, nb0 * P : nb1 * P].rearrange("(p j) n -> p j n", j=4))
+            for nb in range(nb0, nb1):
+                raw[(e, nb)] = t[:, :, (nb - nb0) * P : (nb - nb0 + 1) * P]
+
+        for e in range(E // 2):
+            load_w(e, 0, 2)
+        nc.sync.dma_start(out=bias[:], in_=b.rearrange("(c p) e -> p c e", p=P))
+        for e in range(E // 2, E):
+            load_w(e, 0, 1)
+        nc.sync.dma_start(pos_t[0][:], pos1)
+        nc.sync.dma_start(pos_t[1][:], pos2)
+        for r in range(2):
+            nc.sync.dma_start(out=gates[r][:], in_=gate[r, 0:P, :])
+        for e in range(E // 2, E):
+            load_w(e, 1, 2)
+        for e in range(E):
+            load_w(e, 2, 3)
+
+        gw = []
+        gs = []
+
+        def gather_scales(s0, s1):
+            ts = keep.tile([P, s1 - s0], U8, name="gs%d" % s0, align_bytes=64)
+            nc.vector.tensor_copy(ts[:], xs[:].indirect(offs_t[:, s0 // 16 : s1 // 16]))
+            for s in range(s0, s1, C):
+                gs.append(ts[:, s - s0 : s - s0 + C])
+
+        def gather_words(c, tag):
+            tw = keep.tile([P, GATHER], U32, name="gw%d" % c, tag=tag, align_bytes=64)
+            nc.vector.tensor_copy(tw[:], xw[:].bitcast(U32).indirect(offs_t[:, c * GATHER // 16 : (c + 1) * GATHER // 16]))
+            for s in range(0, GATHER, C):
+                gw.append(tw[:, s : s + C])
+
+        codes = {}
+
+        def quantise(pair):
+            name = "%d_%d" % pair[0]
+            grouped = keep.tile([P, 2 * P, 4], BF16, name="grp" + name, tag="grp" + name, align_bytes=64)
+            for u, (nb, e) in enumerate(pair):
+                nc.scalar.copy(
+                    out=grouped[:, u * P : (u + 1) * P, :].rearrange("p (c i) j -> p c j i", i=4),
+                    in_=raw[(e, nb)].rearrange("p j (c i) -> p c j i", i=4),
+                )
+            wc = keep.tile([P, 2 * P], U32, name="wc" + name, align_bytes=64)
+            ws = keep.tile([P, 2 * P], U8, name="ws" + name, align_bytes=64)
+            nc.vector.quantize_mx(out=wc[:].bitcast(FP8X4), scales=ws[:], in_=grouped[:].rearrange("p n j -> p (n j)"))
+            for u, key in enumerate(pair):
+                codes[key] = (wc[:, u * P : (u + 1) * P], ws[:, u * P : (u + 1) * P])
+
+        def expert(nb, e, y):
+            wc, ws = codes[(nb, e)]
+            acc = psum.tile([P, C], F32, name="acc")
+            nc.tensor.matmul_mx(
+                out=acc[:], lhsT=wc.bitcast(FP8X4), lhsT_scale=ws,
+                rhs=gw[e].bitcast(FP8X4), rhs_scale=gs[e],
+                start=True, stop=True,
+            )
+            nc.scalar.activation(out=y[:, e * C : (e + 1) * C], in_=acc[:], func=RELU, bias=bias[:, nb, e : e + 1])
+
+        def product(nb, y, r, t0, t1):
+            t = keep.tile([P, t1 - t0], F32, name="t%d_%d_%d" % (nb, t0, r))
+            nc.vector.tensor_tensor(t[:], y[:].indirect(pos_t[r][:, t0 // 16 : t1 // 16]), gates[r][:, t0:t1], MULT)
+            return t
+
+        def add_store(nb, t0, t1, a, c, tag):
+            o = keep.tile([P, t1 - t0], F32, name="o%d_%d" % (nb, t0), tag=tag, align_bytes=64)
+            nc.vector.tensor_tensor(o[:], a[:], c[:], ADD)
+            nc.sync.dma_start(out=out[nb * P : (nb + 1) * P, t0:t1], in_=o[:])
+
+        def combine(nb, y, cuts, tag):
+            waiting = None
+            for t0, t1 in zip(cuts[:-1], cuts[1:]):
+                a = product(nb, y, 0, t0, t1)
+                if waiting is not None:
+                    add_store(nb, *waiting)
+                c = product(nb, y, 1, t0, t1)
+                waiting = (t0, t1, a, c, "o%d_%d" % (nb, t0))
+            add_store(nb, waiting[0], waiting[1], waiting[2], waiting[3], tag)
+
+        for s0, s1 in ((0, 768), (768, 1536), (1536, 2048)):
+            gather_scales(s0, s1)
+        gather_words(0, "gw0")
+        quantise([(0, 0), (1, 0)])
+        quantise([(0, 1), (1, 1)])
+        gather_words(1, "grp0_1")
+        quantise([(0, 2), (1, 2)])
+        quantise([(0, 3), (1, 3)])
+        gather_words(2, "grp0_3")
+        quantise([(0, 4), (0, 5)])
+        gather_words(3, "grp0_4")
+        quantise([(0, 6), (0, 7)])
+        for nb in range(NB):
+            y = keep.tile([P, S], F32, name="y%d" % nb, tag="y%d" % nb)
+            for e in range(E):
+                expert(nb, e, y)
+            if nb + 1 < NB:
+                for e in range(E // 2 if nb == 0 else 0, E, 2):
+                    quantise([(nb + 1, e), (nb + 1, e + 1)])
+                combine(nb, y, (0, T), "grp%d_%d" % (nb + 1, E - 2))
+            else:
+                combine(nb, y, (0, 512, 768, T), "last")

@@ -21,7 +21,18 @@ ADD = mybir.AluOpType.add
 RELU = mybir.ActivationFunctionType.Relu
 
 GATHER = 512
-HALF = 512
+WHOLE = 0
+VCAST = 2
+HOLD0 = 1
+TWO = 5
+PAIR = 4
+XW_AFTER = 1
+LAG = 2
+LAG2 = 8
+CUTS = (0, 512, 896, T)
+MID = 768
+HOLDE = 5
+BIAS_AFTER = 2
 
 
 def tile_moe_pkd_lin_relu_kernel(tc, x_words, x_scales, w, b, gate, offs, pos1, pos2, out):
@@ -29,7 +40,7 @@ def tile_moe_pkd_lin_relu_kernel(tc, x_words, x_scales, w, b, gate, offs, pos1, 
     with ExitStack() as ctx:
         lists = ctx.enter_context(tc.tile_pool(name="lists", bufs=1))
         keep = ctx.enter_context(tc.tile_pool(name="keep", bufs=1))
-        psum = ctx.enter_context(tc.psum_pool(name="psum", bufs=8))
+        psum = ctx.enter_context(tc.psum_pool(name="psum", bufs=1))
 
         offs_t = lists.tile([P, S // 16], U16, name="offs_t")
         pos_t = [lists.tile([P, T // 16], U16, name="pos%d_t" % r) for r in range(2)]
@@ -42,31 +53,33 @@ def tile_moe_pkd_lin_relu_kernel(tc, x_words, x_scales, w, b, gate, offs, pos1, 
         nc.sync.dma_start(offs_t[:], offs)
         for q in range(4):
             nc.sync.dma_start(out=xs[32 * q : 32 * q + 4, :].bitcast(I32), in_=x_scales[0, 4 * q : 4 * q + 4, :].bitcast(I32))
-        nc.sync.dma_start(out=xw[:], in_=x_words[0].rearrange("p t r -> p (t r)").bitcast(I32))
 
         raw = {}
 
         def load_w(e, nb0, nb1):
-            width = (nb1 - nb0) * P
-            tag = "y0" if (e, nb0) == (E // 2, 0) else "raw%d_%d" % (e, nb0)
-            t = keep.tile([P, 4, width], F32, name="raw%d_%d" % (e, nb0), tag=tag)
+            t = keep.tile([P, 4, (nb1 - nb0) * P], F32, name="raw%d_%d" % (e, nb0), tag="raw%d_%d" % (e, nb0), align_bytes=64)
             nc.sync.dma_start(out=t[:], in_=w[e, :, nb0 * P : nb1 * P].rearrange("(p j) n -> p j n", j=4))
             for nb in range(nb0, nb1):
-                raw[(e, nb)] = t[:, :, (nb - nb0) * P : (nb - nb0 + 1) * P]
+                raw[e, nb] = (t, nb0)
 
-        for e in range(E // 2):
-            load_w(e, 0, 2)
-        nc.sync.dma_start(out=bias[:], in_=b.rearrange("(c p) e -> p c e", p=P))
-        for e in range(E // 2, E):
-            load_w(e, 0, 1)
-        nc.sync.dma_start(pos_t[0][:], pos1)
-        nc.sync.dma_start(pos_t[1][:], pos2)
-        for r in range(2):
-            nc.sync.dma_start(out=gates[r][:], in_=gate[r, 0:P, :])
-        for e in range(E // 2, E):
-            load_w(e, 1, 2)
+        def first_load(e):
+            return NB if e < WHOLE else 2 if e < TWO else 1
+
         for e in range(E):
-            load_w(e, 2, 3)
+            load_w(e, 0, first_load(e))
+            if e == XW_AFTER:
+                nc.sync.dma_start(out=xw[:], in_=x_words[0].rearrange("p t r -> p (t r)").bitcast(I32))
+            if e == BIAS_AFTER:
+                nc.sync.dma_start(out=bias[:], in_=b.rearrange("(c p) e -> p c e", p=P))
+        nc.sync.dma_start(pos_t[0][:], pos1)
+        nc.sync.dma_start(out=gates[0][:], in_=gate[0, 0:P, :])
+        for nb in range(1, NB):
+            for e in range(E):
+                if first_load(e) <= nb:
+                    load_w(e, nb, nb + 1)
+            if nb == 1:
+                nc.sync.dma_start(pos_t[1][:], pos2)
+                nc.sync.dma_start(out=gates[1][:], in_=gate[1, 0:P, :])
 
         gw = []
         gs = []
@@ -85,23 +98,28 @@ def tile_moe_pkd_lin_relu_kernel(tc, x_words, x_scales, w, b, gate, offs, pos1, 
 
         codes = {}
 
-        def quantise(pair):
-            name = "%d_%d" % pair[0]
-            grouped = keep.tile([P, 2 * P, 4], BF16, name="grp" + name, tag="grp" + name, align_bytes=64)
-            for u, (nb, e) in enumerate(pair):
-                nc.scalar.copy(
-                    out=grouped[:, u * P : (u + 1) * P, :].rearrange("p (c i) j -> p c j i", i=4),
-                    in_=raw[(e, nb)].rearrange("p j (c i) -> p c j i", i=4),
-                )
-            wc = keep.tile([P, 2 * P], U32, name="wc" + name, align_bytes=64)
-            ws = keep.tile([P, 2 * P], U8, name="ws" + name, align_bytes=64)
+        def quantise(e, nb0, nb1, on_vector=False, after=None):
+            name = "%d_%d" % (e, nb0)
+            tile_w, first = raw[e, nb0]
+            width = (nb1 - nb0) * P
+            src = tile_w[:, :, (nb0 - first) * P : (nb1 - first) * P].rearrange("p j (c i) -> p c j i", i=4)
+            grouped = keep.tile([P, width, 4], BF16, name="grp" + name, tag=after or "grp" + name, align_bytes=64)
+            dst = grouped[:].rearrange("p (c i) j -> p c j i", i=4)
+            if on_vector:
+                nc.vector.tensor_copy(out=dst, in_=src)
+            else:
+                nc.scalar.copy(out=dst, in_=src)
+            wc = keep.tile([P, width], U32, name="wc" + name, tag="wc" + name, align_bytes=64)
+            ws = keep.tile([P, width], U8, name="ws" + name, align_bytes=64)
             nc.vector.quantize_mx(out=wc[:].bitcast(FP8X4), scales=ws[:], in_=grouped[:].rearrange("p n j -> p (n j)"))
-            for u, key in enumerate(pair):
-                codes[key] = (wc[:, u * P : (u + 1) * P], ws[:, u * P : (u + 1) * P])
+            for nb in range(nb0, nb1):
+                cols = slice((nb - nb0) * P, (nb - nb0 + 1) * P)
+                codes[nb, e] = (wc[:, cols], ws[:, cols])
 
         def expert(nb, e, y):
             wc, ws = codes[(nb, e)]
-            acc = psum.tile([P, C], F32, name="acc")
+            tag = "bank%d" % (4 * (nb % 2) + e % 4)
+            acc = psum.tile([P, C], F32, name="acc", tag=tag)
             nc.tensor.matmul_mx(
                 out=acc[:], lhsT=wc.bitcast(FP8X4), lhsT_scale=ws,
                 rhs=gw[e].bitcast(FP8X4), rhs_scale=gs[e],
@@ -109,14 +127,15 @@ def tile_moe_pkd_lin_relu_kernel(tc, x_words, x_scales, w, b, gate, offs, pos1, 
             )
             nc.scalar.activation(out=y[:, e * C : (e + 1) * C], in_=acc[:], func=RELU, bias=bias[:, nb, e : e + 1])
 
-        def product(nb, y, r, t0, t1):
-            t = keep.tile([P, t1 - t0], F32, name="t%d_%d_%d" % (nb, t0, r))
+        def product(nb, y, r, t0, t1, tag=None):
+            name = "t%d_%d_%d" % (nb, t0, r)
+            t = keep.tile([P, t1 - t0], F32, name=name, tag=tag or name, align_bytes=64)
             nc.vector.tensor_tensor(t[:], y[:].indirect(pos_t[r][:, t0 // 16 : t1 // 16]), gates[r][:, t0:t1], MULT)
-            return t
+            return t[:]
 
         def add_store(nb, t0, t1, a, c, tag):
             o = keep.tile([P, t1 - t0], F32, name="o%d_%d" % (nb, t0), tag=tag, align_bytes=64)
-            nc.vector.tensor_tensor(o[:], a[:], c[:], ADD)
+            nc.vector.tensor_tensor(o[:], a, c, ADD)
             nc.sync.dma_start(out=out[nb * P : (nb + 1) * P, t0:t1], in_=o[:])
 
         def combine(nb, y, cuts, tag):
@@ -131,23 +150,30 @@ def tile_moe_pkd_lin_relu_kernel(tc, x_words, x_scales, w, b, gate, offs, pos1, 
 
         for s0, s1 in ((0, 768), (768, 1536), (1536, 2048)):
             gather_scales(s0, s1)
-        gather_words(0, "gw0")
-        quantise([(0, 0), (1, 0)])
-        quantise([(0, 1), (1, 1)])
-        gather_words(1, "grp0_1")
-        quantise([(0, 2), (1, 2)])
-        quantise([(0, 3), (1, 3)])
-        gather_words(2, "grp0_3")
-        quantise([(0, 4), (0, 5)])
-        gather_words(3, "grp0_4")
-        quantise([(0, 6), (0, 7)])
-        for nb in range(NB):
-            y = keep.tile([P, S], F32, name="y%d" % nb, tag="y%d" % nb)
-            for e in range(E):
-                expert(nb, e, y)
-            if nb + 1 < NB:
-                for e in range(E // 2 if nb == 0 else 0, E, 2):
-                    quantise([(nb + 1, e), (nb + 1, e + 1)])
-                combine(nb, y, (0, T), "grp%d_%d" % (nb + 1, E - 2))
-            else:
-                combine(nb, y, (0, 512, 768, T), "last")
+        ys = [keep.tile([P, S], F32, name="y%d" % nb) for nb in range(NB)]
+        for e in range(E + LAG):
+            if e < E:
+                quantise(e, 0, 2 if e < PAIR else 1, e >= E - VCAST)
+            if e < S // GATHER:
+                gather_words(e, "raw%d_0" % e if e >= HOLD0 else "gw%d" % e)
+            if e >= LAG:
+                expert(0, e - LAG, ys[0])
+        for e in range(E + LAG2):
+            if PAIR <= e < E:
+                quantise(e, 1, 2, False, "wc%d_0" % max(E - 1 - 2 * (TWO - e), 4) if (e <= TWO) else None)
+            if e >= LAG2:
+                expert(1, e - LAG2, ys[1])
+        a = product(0, ys[0], 0, 0, T)
+        c = product(0, ys[0], 1, 0, T, "raw%d_1" % (E - 1))
+        quantise(0, 2, NB)
+        add_store(0, 0, T, a, c, "raw0_2")
+        for e in range(1, E):
+            quantise(e, 2, NB)
+        for e in range(E):
+            expert(2, e, ys[2])
+        a = product(1, ys[1], 0, 0, T)
+        c0 = product(1, ys[1], 1, 0, MID, "raw%d_2" % HOLDE)
+        c1 = product(1, ys[1], 1, MID, T, "raw%d_2" % (E - 1))
+        add_store(1, 0, MID, a[:, 0:MID], c0, "o1a")
+        add_store(1, MID, T, a[:, MID:T], c1, "o1b")
+        combine(2, ys[2], CUTS, "last")

@@ -1,6 +1,7 @@
 from contextlib import ExitStack
 
 import concourse.mybir as mybir
+from concourse.masks import make_identity
 
 K, T, E, C, N = 512, 1024, 8, 256, 384
 S = E * C
@@ -21,17 +22,13 @@ ADD = mybir.AluOpType.add
 RELU = mybir.ActivationFunctionType.Relu
 
 GATHER = 512
-WHOLE = 0
-VCAST = 2
-HOLD0 = 1
+WHOLE = 2
 TWO = 5
-PAIR = 4
 XW_AFTER = 1
-LAG = 2
 LAG2 = 8
 CUTS = (0, 512, 896, T)
-MID = 768
-HOLDE = 5
+HOLD_A = None
+HOLD_C = "raw7_2"
 BIAS_AFTER = 2
 
 
@@ -53,6 +50,9 @@ def tile_moe_pkd_lin_relu_kernel(tc, x_words, x_scales, w, b, gate, offs, pos1, 
         nc.sync.dma_start(offs_t[:], offs)
         for q in range(4):
             nc.sync.dma_start(out=xs[32 * q : 32 * q + 4, :].bitcast(I32), in_=x_scales[0, 4 * q : 4 * q + 4, :].bitcast(I32))
+
+        ident = keep.tile([P, P], F32, name="ident")
+        make_identity(nc, ident[:])
 
         raw = {}
 
@@ -98,23 +98,23 @@ def tile_moe_pkd_lin_relu_kernel(tc, x_words, x_scales, w, b, gate, offs, pos1, 
 
         codes = {}
 
-        def quantise(e, nb0, nb1, on_vector=False, after=None):
-            name = "%d_%d" % (e, nb0)
-            tile_w, first = raw[e, nb0]
-            width = (nb1 - nb0) * P
-            src = tile_w[:, :, (nb0 - first) * P : (nb1 - first) * P].rearrange("p j (c i) -> p c j i", i=4)
+        def quantise(group, after=None):
+            name = "%d_%d" % group[0]
+            width = len(group) * P
             grouped = keep.tile([P, width, 4], BF16, name="grp" + name, tag=after or "grp" + name, align_bytes=64)
-            dst = grouped[:].rearrange("p (c i) j -> p c j i", i=4)
-            if on_vector:
-                nc.vector.tensor_copy(out=dst, in_=src)
-            else:
-                nc.scalar.copy(out=dst, in_=src)
+            same_expert = all(e == group[0][0] for e, nb in group)
+            for u, (e, nb) in enumerate(group[:1] if same_expert else group):
+                tile_w, first = raw[e, nb]
+                cols = width if same_expert else P
+                nc.scalar.copy(
+                    out=grouped[:, u * P : u * P + cols, :].rearrange("p (c i) j -> p c j i", i=4),
+                    in_=tile_w[:, :, (nb - first) * P : (nb - first) * P + cols].rearrange("p j (c i) -> p c j i", i=4),
+                )
             wc = keep.tile([P, width], U32, name="wc" + name, tag="wc" + name, align_bytes=64)
             ws = keep.tile([P, width], U8, name="ws" + name, align_bytes=64)
             nc.vector.quantize_mx(out=wc[:].bitcast(FP8X4), scales=ws[:], in_=grouped[:].rearrange("p n j -> p (n j)"))
-            for nb in range(nb0, nb1):
-                cols = slice((nb - nb0) * P, (nb - nb0 + 1) * P)
-                codes[nb, e] = (wc[:, cols], ws[:, cols])
+            for u, (e, nb) in enumerate(group):
+                codes[nb, e] = (wc[:, u * P : (u + 1) * P], ws[:, u * P : (u + 1) * P])
 
         def expert(nb, e, y):
             wc, ws = codes[(nb, e)]
@@ -148,32 +148,51 @@ def tile_moe_pkd_lin_relu_kernel(tc, x_words, x_scales, w, b, gate, offs, pos1, 
                 waiting = (t0, t1, a, c, "o%d_%d" % (nb, t0))
             add_store(nb, waiting[0], waiting[1], waiting[2], waiting[3], tag)
 
+        def sum_on_tensor(nb, first, second):
+            for h, t0 in enumerate(range(0, T, 4 * P)):
+                turned = psum.tile([P, 4, P], F32, name="turned", tag="bank%d" % (4 * (1 - nb) + h))
+                for u in range(4):
+                    c = t0 + u * P
+                    nc.tensor.matmul(turned[:, u, :], first[:, c : c + P], ident[:], start=True, stop=False, is_transpose=True)
+                    nc.tensor.matmul(turned[:, u, :], second[:, c : c + P], ident[:], start=False, stop=True, is_transpose=True)
+                z = keep.tile([P, 4, P], F32, name="z%d_%d" % (nb, h))
+                nc.scalar.copy(out=z[:], in_=turned[:])
+                back = psum.tile([P, 4, P], F32, name="back", tag="bank%d" % (4 * (1 - nb) + 2 + h))
+                for u in range(4):
+                    nc.tensor.transpose(back[:, u, :], z[:, u, :], ident[:])
+                o = keep.tile([P, 4, P], F32, name="o%d_%d" % (nb, h))
+                nc.scalar.copy(out=o[:], in_=back[:])
+                nc.scalar.dma_start(out=out[nb * P : (nb + 1) * P, t0 : t0 + 4 * P], in_=o[:].rearrange("p u t -> p (u t)"))
+
         for s0, s1 in ((0, 768), (768, 1536), (1536, 2048)):
             gather_scales(s0, s1)
         ys = [keep.tile([P, S], F32, name="y%d" % nb) for nb in range(NB)]
-        for e in range(E + LAG):
-            if e < E:
-                quantise(e, 0, 2 if e < PAIR else 1, e >= E - VCAST)
-            if e < S // GATHER:
-                gather_words(e, "raw%d_0" % e if e >= HOLD0 else "gw%d" % e)
-            if e >= LAG:
-                expert(0, e - LAG, ys[0])
-        for e in range(E + LAG2):
-            if PAIR <= e < E:
-                quantise(e, 1, 2, False, "wc%d_0" % max(E - 1 - 2 * (TWO - e), 4) if (e <= TWO) else None)
-            if e >= LAG2:
-                expert(1, e - LAG2, ys[1])
-        a = product(0, ys[0], 0, 0, T)
-        c = product(0, ys[0], 1, 0, T, "raw%d_1" % (E - 1))
-        quantise(0, 2, NB)
-        add_store(0, 0, T, a, c, "raw0_2")
-        for e in range(1, E):
-            quantise(e, 2, NB)
+        for e in range(4):
+            quantise([(e, 0), (e, 1)])
+            gather_words(e, "raw%d_0" % e if e >= 1 else "gw0")
+            if e >= 2:
+                expert(0, e - 2, ys[0])
+        quantise([(4, 0), (5, 0)])
+        expert(0, 2, ys[0])
+        expert(0, 3, ys[0])
+        quantise([(6, 0)])
+        quantise([(7, 0)])
+        for e in range(4, E):
+            expert(0, e, ys[0])
+        quantise([(4, 1), (5, 1)], "wc7_0")
+        quantise([(6, 1), (7, 1)])
         for e in range(E):
-            expert(2, e, ys[2])
-        a = product(1, ys[1], 0, 0, T)
-        c0 = product(1, ys[1], 1, 0, MID, "raw%d_2" % HOLDE)
-        c1 = product(1, ys[1], 1, MID, T, "raw%d_2" % (E - 1))
-        add_store(1, 0, MID, a[:, 0:MID], c0, "o1a")
-        add_store(1, MID, T, a[:, MID:T], c1, "o1b")
+            expert(1, e, ys[1])
+        a0 = product(0, ys[0], 0, 0, T)
+        c0 = product(0, ys[0], 1, 0, T, "raw7_1")
+        for e in range(0, E + LAG2, 2):
+            if e < E:
+                quantise([(e, 2), (e + 1, 2)])
+            if e >= LAG2:
+                expert(2, e - LAG2, ys[2])
+                expert(2, e - LAG2 + 1, ys[2])
+        a1 = product(1, ys[1], 0, 0, T, HOLD_A)
+        c1 = product(1, ys[1], 1, 0, T, HOLD_C)
         combine(2, ys[2], CUTS, "last")
+        sum_on_tensor(0, a0, c0)
+        sum_on_tensor(1, a1, c1)

@@ -7,6 +7,7 @@ K, T, E, C, N = 512, 1024, 8, 256, 384
 S = E * C
 P = 128
 NB = N // P
+PACK = 4
 FLOPS = 2 * K * N * S
 BYTES = K * T + 16 * T + 4 * E * K * N + 4 * N * E + 4 * 2 * T + 2 * (S + 2 * T) + 4 * N * T
 
@@ -21,15 +22,18 @@ MULT = mybir.AluOpType.mult
 ADD = mybir.AluOpType.add
 RELU = mybir.ActivationFunctionType.Relu
 
-GATHER = 512
+PER_COLUMN = 16
+SCALE_GATHER = 3 * C
+WORD_GATHER = 2 * C
+BANK = 4 * P
+HALF_E = E // 2
+
 WHOLE = 2
 TWO = 5
-XW_AFTER = 1
-LAG2 = 8
-CUTS = (0, 512, 896, T)
-HOLD_A = None
-HOLD_C = "raw7_2"
+WORDS_AFTER = 1
 BIAS_AFTER = 2
+LAST_CUT = 768
+FREES_FIRST_HALF = 5
 
 
 def tile_moe_pkd_lin_relu_kernel(tc, x_words, x_scales, w, b, gate, offs, pos1, pos2, out):
@@ -39,160 +43,189 @@ def tile_moe_pkd_lin_relu_kernel(tc, x_words, x_scales, w, b, gate, offs, pos1, 
         keep = ctx.enter_context(tc.tile_pool(name="keep", bufs=1))
         psum = ctx.enter_context(tc.psum_pool(name="psum", bufs=1))
 
-        offs_t = lists.tile([P, S // 16], U16, name="offs_t")
-        pos_t = [lists.tile([P, T // 16], U16, name="pos%d_t" % r) for r in range(2)]
-        xw = keep.tile([P, T], I32, name="xw", align_bytes=64)
-        xs = keep.tile([P, T], U8, name="xs", align_bytes=64)
+        offs_t = lists.tile([P, S // PER_COLUMN], U16, name="offs_t")
+        pos_t = [lists.tile([P, T // PER_COLUMN], U16, name="pos%d_t" % r) for r in range(2)]
+        token_words = keep.tile([P, T], I32, name="token_words", align_bytes=64)
+        token_scales = keep.tile([P, T], U8, name="token_scales", align_bytes=64)
         bias = keep.tile([P, NB, E], F32, name="bias")
         gates = [keep.tile([P, T], F32, name="gate%d" % r) for r in range(2)]
 
-        nc.gpsimd.memset(xs[:].bitcast(I32), 0)
+        nc.gpsimd.memset(token_scales[:].bitcast(I32), 0)
         nc.sync.dma_start(offs_t[:], offs)
         for q in range(4):
-            nc.sync.dma_start(out=xs[32 * q : 32 * q + 4, :].bitcast(I32), in_=x_scales[0, 4 * q : 4 * q + 4, :].bitcast(I32))
+            nc.sync.dma_start(
+                out=token_scales[32 * q : 32 * q + 4, :].bitcast(I32),
+                in_=x_scales[0, 4 * q : 4 * q + 4, :].bitcast(I32),
+            )
 
         ident = keep.tile([P, P], F32, name="ident")
         make_identity(nc, ident[:])
 
-        raw = {}
+        loaded = {}
+
+        def loaded_tag(e, nb):
+            return "w%d_%d" % (e, nb)
 
         def load_w(e, nb0, nb1):
-            t = keep.tile([P, 4, (nb1 - nb0) * P], F32, name="raw%d_%d" % (e, nb0), tag="raw%d_%d" % (e, nb0), align_bytes=64)
-            nc.sync.dma_start(out=t[:], in_=w[e, :, nb0 * P : nb1 * P].rearrange("(p j) n -> p j n", j=4))
+            t = keep.tile([P, PACK, (nb1 - nb0) * P], F32, name=loaded_tag(e, nb0), tag=loaded_tag(e, nb0), align_bytes=64)
+            nc.sync.dma_start(out=t[:], in_=w[e, :, nb0 * P : nb1 * P].rearrange("(p j) n -> p j n", j=PACK))
             for nb in range(nb0, nb1):
-                raw[e, nb] = (t, nb0)
+                loaded[e, nb] = (t, nb0)
 
-        def first_load(e):
+        def blocks_in_first_load(e):
             return NB if e < WHOLE else 2 if e < TWO else 1
 
         for e in range(E):
-            load_w(e, 0, first_load(e))
-            if e == XW_AFTER:
-                nc.sync.dma_start(out=xw[:], in_=x_words[0].rearrange("p t r -> p (t r)").bitcast(I32))
+            load_w(e, 0, blocks_in_first_load(e))
+            if e == WORDS_AFTER:
+                nc.sync.dma_start(out=token_words[:], in_=x_words[0].rearrange("p t r -> p (t r)").bitcast(I32))
             if e == BIAS_AFTER:
                 nc.sync.dma_start(out=bias[:], in_=b.rearrange("(c p) e -> p c e", p=P))
         nc.sync.dma_start(pos_t[0][:], pos1)
         nc.sync.dma_start(out=gates[0][:], in_=gate[0, 0:P, :])
         for nb in range(1, NB):
             for e in range(E):
-                if first_load(e) <= nb:
+                if blocks_in_first_load(e) <= nb:
                     load_w(e, nb, nb + 1)
             if nb == 1:
                 nc.sync.dma_start(pos_t[1][:], pos2)
                 nc.sync.dma_start(out=gates[1][:], in_=gate[1, 0:P, :])
 
-        gw = []
-        gs = []
+        slot_words = []
+        slot_scales = []
 
         def gather_scales(s0, s1):
-            ts = keep.tile([P, s1 - s0], U8, name="gs%d" % s0, align_bytes=64)
-            nc.vector.tensor_copy(ts[:], xs[:].indirect(offs_t[:, s0 // 16 : s1 // 16]))
-            for s in range(s0, s1, C):
-                gs.append(ts[:, s - s0 : s - s0 + C])
+            t = keep.tile([P, s1 - s0], U8, name="slot_scales%d" % s0, align_bytes=64)
+            nc.vector.tensor_copy(t[:], token_scales[:].indirect(offs_t[:, s0 // PER_COLUMN : s1 // PER_COLUMN]))
+            for s in range(0, s1 - s0, C):
+                slot_scales.append(t[:, s : s + C])
 
-        def gather_words(c, tag):
-            tw = keep.tile([P, GATHER], U32, name="gw%d" % c, tag=tag, align_bytes=64)
-            nc.vector.tensor_copy(tw[:], xw[:].bitcast(U32).indirect(offs_t[:, c * GATHER // 16 : (c + 1) * GATHER // 16]))
-            for s in range(0, GATHER, C):
-                gw.append(tw[:, s : s + C])
+        def gather_words(piece, after=None):
+            name = "slot_words%d" % piece
+            s0, s1 = piece * WORD_GATHER, (piece + 1) * WORD_GATHER
+            t = keep.tile([P, WORD_GATHER], U32, name=name, tag=after or name, align_bytes=64)
+            nc.vector.tensor_copy(
+                t[:], token_words[:].bitcast(U32).indirect(offs_t[:, s0 // PER_COLUMN : s1 // PER_COLUMN])
+            )
+            for s in range(0, WORD_GATHER, C):
+                slot_words.append(t[:, s : s + C])
 
-        codes = {}
+        weights = {}
+
+        def words_tag(e, nb):
+            return "w_words%d_%d" % (e, nb)
 
         def quantise(group, after=None):
             name = "%d_%d" % group[0]
             width = len(group) * P
-            grouped = keep.tile([P, width, 4], BF16, name="grp" + name, tag=after or "grp" + name, align_bytes=64)
-            same_expert = all(e == group[0][0] for e, nb in group)
-            for u, (e, nb) in enumerate(group[:1] if same_expert else group):
-                tile_w, first = raw[e, nb]
-                cols = width if same_expert else P
+            rounded = keep.tile([P, width, PACK], BF16, name="rounded" + name, tag=after or "rounded" + name, align_bytes=64)
+            one_expert = all(e == group[0][0] for e, nb in group)
+            cols = width if one_expert else P
+            for u, (e, nb) in enumerate(group[:1] if one_expert else group):
+                t, first = loaded[e, nb]
                 nc.scalar.copy(
-                    out=grouped[:, u * P : u * P + cols, :].rearrange("p (c i) j -> p c j i", i=4),
-                    in_=tile_w[:, :, (nb - first) * P : (nb - first) * P + cols].rearrange("p j (c i) -> p c j i", i=4),
+                    out=rounded[:, u * P : u * P + cols, :].rearrange("p (c i) j -> p c j i", i=4),
+                    in_=t[:, :, (nb - first) * P : (nb - first) * P + cols].rearrange("p j (c i) -> p c j i", i=4),
                 )
-            wc = keep.tile([P, width], U32, name="wc" + name, tag="wc" + name, align_bytes=64)
-            ws = keep.tile([P, width], U8, name="ws" + name, align_bytes=64)
-            nc.vector.quantize_mx(out=wc[:].bitcast(FP8X4), scales=ws[:], in_=grouped[:].rearrange("p n j -> p (n j)"))
-            for u, (e, nb) in enumerate(group):
-                codes[nb, e] = (wc[:, u * P : (u + 1) * P], ws[:, u * P : (u + 1) * P])
+            words = keep.tile([P, width], U32, name=words_tag(*group[0]), tag=words_tag(*group[0]), align_bytes=64)
+            scales = keep.tile([P, width], U8, name="w_scales" + name, align_bytes=64)
+            nc.vector.quantize_mx(
+                out=words[:].bitcast(FP8X4), scales=scales[:], in_=rounded[:].rearrange("p n j -> p (n j)")
+            )
+            for u, key in enumerate(group):
+                weights[key] = (words[:, u * P : (u + 1) * P], scales[:, u * P : (u + 1) * P])
 
-        def expert(nb, e, y):
-            wc, ws = codes[(nb, e)]
-            tag = "bank%d" % (4 * (nb % 2) + e % 4)
-            acc = psum.tile([P, C], F32, name="acc", tag=tag)
+        def expert(e, nb, y):
+            words, scales = weights[e, nb]
+            acc = psum.tile([P, C], F32, name="acc", tag="bank%d" % (4 * (nb % 2) + e % 4))
             nc.tensor.matmul_mx(
-                out=acc[:], lhsT=wc.bitcast(FP8X4), lhsT_scale=ws,
-                rhs=gw[e].bitcast(FP8X4), rhs_scale=gs[e],
-                start=True, stop=True,
+                out=acc[:],
+                lhsT=words.bitcast(FP8X4),
+                lhsT_scale=scales,
+                rhs=slot_words[e].bitcast(FP8X4),
+                rhs_scale=slot_scales[e],
+                start=True,
+                stop=True,
             )
             nc.scalar.activation(out=y[:, e * C : (e + 1) * C], in_=acc[:], func=RELU, bias=bias[:, nb, e : e + 1])
 
-        def product(nb, y, r, t0, t1, tag=None):
-            name = "t%d_%d_%d" % (nb, t0, r)
-            t = keep.tile([P, t1 - t0], F32, name=name, tag=tag or name, align_bytes=64)
-            nc.vector.tensor_tensor(t[:], y[:].indirect(pos_t[r][:, t0 // 16 : t1 // 16]), gates[r][:, t0:t1], MULT)
+        def product(nb, y, r, t0, t1, after=None):
+            name = "product%d_%d_%d" % (nb, t0, r)
+            t = keep.tile([P, t1 - t0], F32, name=name, tag=after or name, align_bytes=64)
+            fetched = y[:].indirect(pos_t[r][:, t0 // PER_COLUMN : t1 // PER_COLUMN])
+            nc.vector.tensor_tensor(t[:], fetched, gates[r][:, t0:t1], MULT)
             return t[:]
 
-        def add_store(nb, t0, t1, a, c, tag):
-            o = keep.tile([P, t1 - t0], F32, name="o%d_%d" % (nb, t0), tag=tag, align_bytes=64)
-            nc.vector.tensor_tensor(o[:], a, c, ADD)
-            nc.sync.dma_start(out=out[nb * P : (nb + 1) * P, t0:t1], in_=o[:])
+        def sum_on_vector(nb, t0, t1, first, second):
+            total = keep.tile([P, t1 - t0], F32, name="total%d_%d" % (nb, t0), align_bytes=64)
+            nc.vector.tensor_tensor(total[:], first, second, ADD)
+            nc.sync.dma_start(out=out[nb * P : (nb + 1) * P, t0:t1], in_=total[:])
 
-        def combine(nb, y, cuts, tag):
-            waiting = None
-            for t0, t1 in zip(cuts[:-1], cuts[1:]):
-                a = product(nb, y, 0, t0, t1)
-                if waiting is not None:
-                    add_store(nb, *waiting)
-                c = product(nb, y, 1, t0, t1)
-                waiting = (t0, t1, a, c, "o%d_%d" % (nb, t0))
-            add_store(nb, waiting[0], waiting[1], waiting[2], waiting[3], tag)
-
-        def sum_on_tensor(nb, first, second):
-            for h, t0 in enumerate(range(0, T, 4 * P)):
-                turned = psum.tile([P, 4, P], F32, name="turned", tag="bank%d" % (4 * (1 - nb) + h))
+        def sum_on_tensor(nb, first, second_halves):
+            bank0 = 4 * (1 - nb)
+            for h, second in enumerate(second_halves):
+                t0 = h * BANK
+                turned = psum.tile([P, 4, P], F32, name="turned", tag="bank%d" % (bank0 + h))
                 for u in range(4):
-                    c = t0 + u * P
-                    nc.tensor.matmul(turned[:, u, :], first[:, c : c + P], ident[:], start=True, stop=False, is_transpose=True)
-                    nc.tensor.matmul(turned[:, u, :], second[:, c : c + P], ident[:], start=False, stop=True, is_transpose=True)
-                z = keep.tile([P, 4, P], F32, name="z%d_%d" % (nb, h))
-                nc.scalar.copy(out=z[:], in_=turned[:])
-                back = psum.tile([P, 4, P], F32, name="back", tag="bank%d" % (4 * (1 - nb) + 2 + h))
+                    cols = slice(u * P, (u + 1) * P)
+                    first_half = first[:, t0 : t0 + BANK]
+                    nc.tensor.matmul(turned[:, u, :], first_half[:, cols], ident[:], start=True, stop=False, is_transpose=True)
+                    nc.tensor.matmul(turned[:, u, :], second[:, cols], ident[:], start=False, stop=True, is_transpose=True)
+                turned_sum = keep.tile([P, 4, P], F32, name="turned_sum%d_%d" % (nb, h))
+                nc.scalar.copy(out=turned_sum[:], in_=turned[:])
+                back = psum.tile([P, 4, P], F32, name="back", tag="bank%d" % (bank0 + 2 + h))
                 for u in range(4):
-                    nc.tensor.transpose(back[:, u, :], z[:, u, :], ident[:])
-                o = keep.tile([P, 4, P], F32, name="o%d_%d" % (nb, h))
-                nc.scalar.copy(out=o[:], in_=back[:])
-                nc.scalar.dma_start(out=out[nb * P : (nb + 1) * P, t0 : t0 + 4 * P], in_=o[:].rearrange("p u t -> p (u t)"))
+                    nc.tensor.transpose(back[:, u, :], turned_sum[:, u, :], ident[:])
+                total = keep.tile([P, 4, P], F32, name="total%d_%d" % (nb, h))
+                nc.scalar.copy(out=total[:], in_=back[:])
+                nc.scalar.dma_start(
+                    out=out[nb * P : (nb + 1) * P, t0 : t0 + BANK], in_=total[:].rearrange("p u t -> p (u t)")
+                )
 
-        for s0, s1 in ((0, 768), (768, 1536), (1536, 2048)):
-            gather_scales(s0, s1)
+        for s0 in range(0, S, SCALE_GATHER):
+            gather_scales(s0, min(s0 + SCALE_GATHER, S))
         ys = [keep.tile([P, S], F32, name="y%d" % nb) for nb in range(NB)]
-        for e in range(4):
+
+        lag = 2
+        for e in range(HALF_E):
             quantise([(e, 0), (e, 1)])
-            gather_words(e, "raw%d_0" % e if e >= 1 else "gw0")
-            if e >= 2:
-                expert(0, e - 2, ys[0])
-        quantise([(4, 0), (5, 0)])
-        expert(0, 2, ys[0])
-        expert(0, 3, ys[0])
-        quantise([(6, 0)])
-        quantise([(7, 0)])
-        for e in range(4, E):
-            expert(0, e, ys[0])
-        quantise([(4, 1), (5, 1)], "wc7_0")
-        quantise([(6, 1), (7, 1)])
+            gather_words(e, loaded_tag(e, 0) if e > 0 else None)
+            if e >= lag:
+                expert(e - lag, 0, ys[0])
+        quantise([(HALF_E, 0), (HALF_E + 1, 0)])
+        for e in range(HALF_E - lag, HALF_E):
+            expert(e, 0, ys[0])
+        quantise([(E - 2, 0)])
+        quantise([(E - 1, 0)])
+        for e in range(HALF_E, E):
+            expert(e, 0, ys[0])
+
+        quantise([(HALF_E, 1), (HALF_E + 1, 1)], words_tag(E - 1, 0))
+        quantise([(E - 2, 1), (E - 1, 1)])
         for e in range(E):
-            expert(1, e, ys[1])
-        a0 = product(0, ys[0], 0, 0, T)
-        c0 = product(0, ys[0], 1, 0, T, "raw7_1")
-        for e in range(0, E + LAG2, 2):
-            if e < E:
-                quantise([(e, 2), (e + 1, 2)])
-            if e >= LAG2:
-                expert(2, e - LAG2, ys[2])
-                expert(2, e - LAG2 + 1, ys[2])
-        a1 = product(1, ys[1], 0, 0, T, HOLD_A)
-        c1 = product(1, ys[1], 1, 0, T, HOLD_C)
-        combine(2, ys[2], CUTS, "last")
-        sum_on_tensor(0, a0, c0)
-        sum_on_tensor(1, a1, c1)
+            expert(e, 1, ys[1])
+
+        first0 = product(0, ys[0], 0, 0, T)
+        second0 = product(0, ys[0], 1, 0, T, loaded_tag(E - 1, 1))
+
+        group_cuts = (0, WHOLE, FREES_FIRST_HALF + 1, E)
+        for e0, e1 in zip(group_cuts[:-1], group_cuts[1:]):
+            quantise([(e, 2) for e in range(e0, e1)])
+        for e in range(E):
+            expert(e, 2, ys[2])
+
+        first1 = product(1, ys[1], 0, 0, T)
+        second1 = [
+            product(1, ys[1], 1, 0, BANK, loaded_tag(FREES_FIRST_HALF, 2)),
+            product(1, ys[1], 1, BANK, T, loaded_tag(E - 1, 2)),
+        ]
+
+        first2 = product(2, ys[2], 0, 0, LAST_CUT)
+        second2 = product(2, ys[2], 1, 0, LAST_CUT)
+        first_end = product(2, ys[2], 0, LAST_CUT, T)
+        sum_on_vector(2, 0, LAST_CUT, first2, second2)
+        second_end = product(2, ys[2], 1, LAST_CUT, T)
+        sum_on_vector(2, LAST_CUT, T, first_end, second_end)
+
+        sum_on_tensor(0, first0, [second0[:, 0:BANK], second0[:, BANK:T]])
+        sum_on_tensor(1, first1, second1)

from contextlib import ExitStack

import concourse.mybir as mybir
from concourse.masks import make_identity

K, T, E, C, N = 512, 1024, 8, 256, 384
S = E * C
P = 128
NB = N // P
PACK = 4
FLOPS = 2 * K * N * S
BYTES = K * T + 16 * T + 4 * E * K * N + 4 * N * E + 4 * 2 * T + 2 * (S + 2 * T) + 4 * N * T

F32 = mybir.dt.float32
BF16 = mybir.dt.bfloat16
I32 = mybir.dt.int32
U32 = mybir.dt.uint32
U16 = mybir.dt.uint16
U8 = mybir.dt.uint8
FP8X4 = mybir.dt.float8_e4m3fn_x4
MULT = mybir.AluOpType.mult
ADD = mybir.AluOpType.add
RELU = mybir.ActivationFunctionType.Relu

PER_COLUMN = 16
SCALE_GATHER = 3 * C
WORD_GATHER = 2 * C
BANK = 4 * P
HALF_E = E // 2

WHOLE = 2
TWO = 5
WORDS_AFTER = 1
BIAS_AFTER = 2
LAST_CUT = 768
FREES_FIRST_HALF = 5


def tile_moe_pkd_lin_relu_kernel(tc, x_words, x_scales, w, b, gate, offs, pos1, pos2, out):
    nc = tc.nc
    with ExitStack() as ctx:
        lists = ctx.enter_context(tc.tile_pool(name="lists", bufs=1))
        keep = ctx.enter_context(tc.tile_pool(name="keep", bufs=1))
        psum = ctx.enter_context(tc.psum_pool(name="psum", bufs=1))

        offs_t = lists.tile([P, S // PER_COLUMN], U16, name="offs_t")
        pos_t = [lists.tile([P, T // PER_COLUMN], U16, name="pos%d_t" % r) for r in range(2)]
        token_words = keep.tile([P, T], I32, name="token_words", align_bytes=64)
        token_scales = keep.tile([P, T], U8, name="token_scales", align_bytes=64)
        bias = keep.tile([P, NB, E], F32, name="bias")
        gates = [keep.tile([P, T], F32, name="gate%d" % r) for r in range(2)]

        nc.gpsimd.memset(token_scales[:].bitcast(I32), 0)
        nc.sync.dma_start(offs_t[:], offs)
        for q in range(4):
            nc.sync.dma_start(
                out=token_scales[32 * q : 32 * q + 4, :].bitcast(I32),
                in_=x_scales[0, 4 * q : 4 * q + 4, :].bitcast(I32),
            )

        ident = keep.tile([P, P], F32, name="ident")
        make_identity(nc, ident[:])

        loaded = {}

        def loaded_tag(e, nb):
            return "w%d_%d" % (e, nb)

        def load_w(e, nb0, nb1):
            t = keep.tile([P, PACK, (nb1 - nb0) * P], F32, name=loaded_tag(e, nb0), tag=loaded_tag(e, nb0), align_bytes=64)
            nc.sync.dma_start(out=t[:], in_=w[e, :, nb0 * P : nb1 * P].rearrange("(p j) n -> p j n", j=PACK))
            for nb in range(nb0, nb1):
                loaded[e, nb] = (t, nb0)

        def blocks_in_first_load(e):
            return NB if e < WHOLE else 2 if e < TWO else 1

        for e in range(E):
            load_w(e, 0, blocks_in_first_load(e))
            if e == WORDS_AFTER:
                nc.sync.dma_start(out=token_words[:], in_=x_words[0].rearrange("p t r -> p (t r)").bitcast(I32))
            if e == BIAS_AFTER:
                nc.sync.dma_start(out=bias[:], in_=b.rearrange("(c p) e -> p c e", p=P))
        nc.sync.dma_start(pos_t[0][:], pos1)
        nc.sync.dma_start(out=gates[0][:], in_=gate[0, 0:P, :])
        for nb in range(1, NB):
            for e in range(E):
                if blocks_in_first_load(e) <= nb:
                    load_w(e, nb, nb + 1)
            if nb == 1:
                nc.sync.dma_start(pos_t[1][:], pos2)
                nc.sync.dma_start(out=gates[1][:], in_=gate[1, 0:P, :])

        slot_words = []
        slot_scales = []

        def gather_scales(s0, s1):
            t = keep.tile([P, s1 - s0], U8, name="slot_scales%d" % s0, align_bytes=64)
            nc.vector.tensor_copy(t[:], token_scales[:].indirect(offs_t[:, s0 // PER_COLUMN : s1 // PER_COLUMN]))
            for s in range(0, s1 - s0, C):
                slot_scales.append(t[:, s : s + C])

        def gather_words(piece, after=None):
            name = "slot_words%d" % piece
            s0, s1 = piece * WORD_GATHER, (piece + 1) * WORD_GATHER
            t = keep.tile([P, WORD_GATHER], U32, name=name, tag=after or name, align_bytes=64)
            nc.vector.tensor_copy(
                t[:], token_words[:].bitcast(U32).indirect(offs_t[:, s0 // PER_COLUMN : s1 // PER_COLUMN])
            )
            for s in range(0, WORD_GATHER, C):
                slot_words.append(t[:, s : s + C])

        weights = {}

        def words_tag(e, nb):
            return "w_words%d_%d" % (e, nb)

        def quantise(group, after=None):
            name = "%d_%d" % group[0]
            width = len(group) * P
            rounded = keep.tile([P, width, PACK], BF16, name="rounded" + name, tag=after or "rounded" + name, align_bytes=64)
            one_expert = all(e == group[0][0] for e, nb in group)
            cols = width if one_expert else P
            for u, (e, nb) in enumerate(group[:1] if one_expert else group):
                t, first = loaded[e, nb]
                nc.scalar.copy(
                    out=rounded[:, u * P : u * P + cols, :].rearrange("p (c i) j -> p c j i", i=4),
                    in_=t[:, :, (nb - first) * P : (nb - first) * P + cols].rearrange("p j (c i) -> p c j i", i=4),
                )
            words = keep.tile([P, width], U32, name=words_tag(*group[0]), tag=words_tag(*group[0]), align_bytes=64)
            scales = keep.tile([P, width], U8, name="w_scales" + name, align_bytes=64)
            nc.vector.quantize_mx(
                out=words[:].bitcast(FP8X4), scales=scales[:], in_=rounded[:].rearrange("p n j -> p (n j)")
            )
            for u, key in enumerate(group):
                weights[key] = (words[:, u * P : (u + 1) * P], scales[:, u * P : (u + 1) * P])

        def expert(e, nb, y):
            words, scales = weights[e, nb]
            acc = psum.tile([P, C], F32, name="acc", tag="bank%d" % (4 * (nb % 2) + e % 4))
            nc.tensor.matmul_mx(
                out=acc[:],
                lhsT=words.bitcast(FP8X4),
                lhsT_scale=scales,
                rhs=slot_words[e].bitcast(FP8X4),
                rhs_scale=slot_scales[e],
                start=True,
                stop=True,
            )
            nc.scalar.activation(out=y[:, e * C : (e + 1) * C], in_=acc[:], func=RELU, bias=bias[:, nb, e : e + 1])

        def product(nb, y, r, t0, t1, after=None):
            name = "product%d_%d_%d" % (nb, t0, r)
            t = keep.tile([P, t1 - t0], F32, name=name, tag=after or name, align_bytes=64)
            fetched = y[:].indirect(pos_t[r][:, t0 // PER_COLUMN : t1 // PER_COLUMN])
            nc.vector.tensor_tensor(t[:], fetched, gates[r][:, t0:t1], MULT)
            return t[:]

        def sum_on_vector(nb, t0, t1, first, second):
            total = keep.tile([P, t1 - t0], F32, name="total%d_%d" % (nb, t0), align_bytes=64)
            nc.vector.tensor_tensor(total[:], first, second, ADD)
            nc.sync.dma_start(out=out[nb * P : (nb + 1) * P, t0:t1], in_=total[:])

        def sum_on_tensor(nb, first, second_halves):
            bank0 = 4 * (1 - nb)
            for h, second in enumerate(second_halves):
                t0 = h * BANK
                turned = psum.tile([P, 4, P], F32, name="turned", tag="bank%d" % (bank0 + h))
                for u in range(4):
                    cols = slice(u * P, (u + 1) * P)
                    first_half = first[:, t0 : t0 + BANK]
                    nc.tensor.matmul(turned[:, u, :], first_half[:, cols], ident[:], start=True, stop=False, is_transpose=True)
                    nc.tensor.matmul(turned[:, u, :], second[:, cols], ident[:], start=False, stop=True, is_transpose=True)
                turned_sum = keep.tile([P, 4, P], F32, name="turned_sum%d_%d" % (nb, h))
                nc.scalar.copy(out=turned_sum[:], in_=turned[:])
                back = psum.tile([P, 4, P], F32, name="back", tag="bank%d" % (bank0 + 2 + h))
                for u in range(4):
                    nc.tensor.transpose(back[:, u, :], turned_sum[:, u, :], ident[:])
                total = keep.tile([P, 4, P], F32, name="total%d_%d" % (nb, h))
                nc.scalar.copy(out=total[:], in_=back[:])
                nc.scalar.dma_start(
                    out=out[nb * P : (nb + 1) * P, t0 : t0 + BANK], in_=total[:].rearrange("p u t -> p (u t)")
                )

        for s0 in range(0, S, SCALE_GATHER):
            gather_scales(s0, min(s0 + SCALE_GATHER, S))
        ys = [keep.tile([P, S], F32, name="y%d" % nb) for nb in range(NB)]

        lag = 2
        for e in range(HALF_E):
            quantise([(e, 0), (e, 1)])
            gather_words(e, loaded_tag(e, 0) if e > 0 else None)
            if e >= lag:
                expert(e - lag, 0, ys[0])
        quantise([(HALF_E, 0), (HALF_E + 1, 0)])
        for e in range(HALF_E - lag, HALF_E):
            expert(e, 0, ys[0])
        quantise([(E - 2, 0)])
        quantise([(E - 1, 0)])
        for e in range(HALF_E, E):
            expert(e, 0, ys[0])

        quantise([(HALF_E, 1), (HALF_E + 1, 1)], words_tag(E - 1, 0))
        quantise([(E - 2, 1), (E - 1, 1)])
        for e in range(E):
            expert(e, 1, ys[1])

        first0 = product(0, ys[0], 0, 0, T)
        second0 = product(0, ys[0], 1, 0, T, loaded_tag(E - 1, 1))

        group_cuts = (0, WHOLE, FREES_FIRST_HALF + 1, E)
        for e0, e1 in zip(group_cuts[:-1], group_cuts[1:]):
            quantise([(e, 2) for e in range(e0, e1)])
        for e in range(E):
            expert(e, 2, ys[2])

        first1 = product(1, ys[1], 0, 0, T)
        second1 = [
            product(1, ys[1], 1, 0, BANK, loaded_tag(FREES_FIRST_HALF, 2)),
            product(1, ys[1], 1, BANK, T, loaded_tag(E - 1, 2)),
        ]

        first2 = product(2, ys[2], 0, 0, LAST_CUT)
        second2 = product(2, ys[2], 1, 0, LAST_CUT)
        first_end = product(2, ys[2], 0, LAST_CUT, T)
        sum_on_vector(2, 0, LAST_CUT, first2, second2)
        second_end = product(2, ys[2], 1, LAST_CUT, T)
        sum_on_vector(2, LAST_CUT, T, first_end, second_end)

        sum_on_tensor(0, first0, [second0[:, 0:BANK], second0[:, BANK:T]])
        sum_on_tensor(1, first1, second1)
